import numpy as np
CORES = [6,14,22,30,134,142,150,158,262,270,278,286,390,398,406,414]
N = 16
def setup_inputs(rng):
    return {"x1": rng.standard_normal((N, 128, 64), dtype=np.float32), "x2": rng.standard_normal((N, 128, 1), dtype=np.float32), "x3": rng.standard_normal((N, 128, 256), dtype=np.float32), "x4": rng.standard_normal((N, 128, 16), dtype=np.float32)}
def reference(x1, x2, x3, x4):
    out = {}
    s = x1.sum(axis=0, dtype=np.float64).astype(x1.dtype)
    out["y1"] = np.broadcast_to(s, (N,) + s.shape)
    s = x2.sum(axis=0, dtype=np.float64).astype(x2.dtype)
    out["y2"] = np.broadcast_to(s, (N,) + s.shape)
    s = x3.sum(axis=0, dtype=np.float64).astype(x3.dtype)
    out["y3"] = np.broadcast_to(s, (N,) + s.shape)
    s = x4.sum(axis=0, dtype=np.float64).astype(x4.dtype)
    out["y4"] = np.broadcast_to(s, (N,) + s.shape)
    return out

@@ -1,0 +1,95 @@
+from concourse.bass import DstId, RemoteDMATransfer
+
+U = 32
+NU = 11
+
+SCRATCH = {
+    "pack": ("dram", [NU, 128, U], "float32"),
+    "land": ("dram", [NU, 128, U], "float32"),
+}
+SEMAPHORES = ["ld3", "lds", "sent", "in1", "in2", "a3", "a1", "a4", "st"]
+
+PLACE = [(0, 0, 0), (0, 1, 1), (0, 2, 0), (0, 3, 1), (1, 0, 0), (1, 1, 1), (1, 2, 0), (1, 3, 1),
+         (0, 4, 0), (1, 5, 1), (0, 6, 1)]
+
+
+def helpers(u, rack):
+    slot, chip, die = PLACE[u]
+    base = (slot if rack == 0 else 3 - slot) * 128 + chip * 8
+    return (base + 5, base + 7) if die == 0 else (base + 1, base + 3)
+
+
+def sends(c, rack):
+    big, i = [], 0
+    for u in range(8):
+        if helpers(u, rack)[0] // 8 == c // 8:
+            big.append((u, 0xFF00))
+        else:
+            big.append((u, (1 << i) if i < 6 else 0xC0))
+            i += 1
+    return [big, [(8, 0x0F), (9, 0x30), (10, 0xC0)]]
+
+
+def bits(m):
+    return bin(m).count("1")
+
+
+def rank_program(g, core, T, topo):
+    rack = topo.rack(topo.host(core))
+    peers = [c for c in T.cores if topo.rack(topo.host(c)) == rack]
+    S = T.sem
+
+    def did(dst):
+        rid, pid = topo.addr(dst, core)
+        return DstId(rid=rid, pnc=pid)
+
+    if T.rank_of(core) is not None:
+        k = peers.index(core)
+        g.sync.dma_start(T.pack[0:8], T.x3[:]).then_inc(S.ld3, 16)
+        g.scalar.dma_start(T.pack[8:10], T.x1[:]).then_inc(S.lds, 16)
+        g.sync.dma_start(T.pack[10, 0:64, :], T.x4[:]).then_inc(S.lds, 16)
+        g.scalar.dma_start(T.pack[10, 64:68, :], T.x2[:]).then_inc(S.lds, 16)
+        g.scalar.dma_start(T.pack[10, 68:128, :], T.x4[0:120, :]).then_inc(S.lds, 16)
+        out = 0
+        for n, call in enumerate(sends(core, rack)):
+            if n == 0:
+                g.wait_ge(S.ld3, 16)
+            else:
+                g.wait_ge(S.lds, 64)
+            g.remote_dma_fused(
+                [RemoteDMATransfer(dst_ids=[did(helpers(u, rack)[0])], dma_engine_mask=m, remote_sem=S.in1,
+                                   src=T.pack[u], dst=T.land[k]) for u, m in call],
+                local_sem=S.sent)
+            out += sum(bits(m) for u, m in call)
+        g.sync.wait_ge(S.a3, 64)
+        g.sync.dma_start(T.y3[:], T.land[0:8]).then_inc(S.st, 16)
+        g.scalar.wait_ge(S.a1, 16)
+        g.scalar.dma_start(T.y1[:], T.land[8:10]).then_inc(S.st, 16)
+        g.scalar.wait_ge(S.a4, 8)
+        g.scalar.dma_start(T.y4[:], T.land[10, 0:64, :]).then_inc(S.st, 16)
+        g.scalar.dma_start(T.y2[:], T.land[10, 64:68, :]).then_inc(S.st, 16)
+        g.wait_ge(S.sent, out)
+        g.wait_ge(S.a3, 64)
+        g.wait_ge(S.a1, 16)
+        g.wait_ge(S.a4, 8)
+        g.wait_ge(S.st, 64)
+        return
+
+    for u in range(NU):
+        a, b = helpers(u, rack)
+        if core == a:
+            need = sum(bits(m) for c in peers for call in sends(c, rack) for v, m in call if v == u)
+            g.wait_ge(S.in1, need)
+            g.remote_dma_fused(
+                [RemoteDMATransfer(dst_ids=[did(b), did(helpers(u, 1 - rack)[1])], dma_engine_mask=0xFF, remote_sem=S.in2,
+                                   srcs=[T.land[j] for j in range(8)], dsts=[T.land[0], T.land[1]], alu_op=1)],
+                local_sem=S.sent)
+            g.wait_ge(S.sent, 8)
+        elif core == b:
+            arr = S.a3 if u < 8 else (S.a1 if u < 10 else S.a4)
+            g.wait_ge(S.in2, 16)
+            g.remote_dma_fused(
+                [RemoteDMATransfer(dst_ids=[did(c) for c in peers], dma_engine_mask=0xFF, remote_sem=arr,
+                                   srcs=[T.land[0], T.land[1]], dsts=[T.land[u] for c in peers], alu_op=1)],
+                local_sem=S.sent)
+            g.wait_ge(S.sent, 8)

@@ -1,7 +1,7 @@
 from concourse.bass import DstId, RemoteDMATransfer
 
-U = 32
-NU = 11
+U = 16
+NU = 22
 
 SCRATCH = {
     "pack": ("dram", [NU, 128, U], "float32"),
@@ -9,8 +9,8 @@ SCRATCH = {
 }
 SEMAPHORES = ["ld3", "lds", "sent", "in1", "in2", "a3", "a1", "a4", "st"]
 
-PLACE = [(0, 0, 0), (0, 1, 1), (0, 2, 0), (0, 3, 1), (1, 0, 0), (1, 1, 1), (1, 2, 0), (1, 3, 1),
-         (0, 4, 0), (1, 5, 1), (0, 6, 1)]
+PLACE = [(s, c, d) for s in (0, 1) for c in (0, 1, 2, 3) for d in (0, 1)] + \
+        [(0, 4, 0), (1, 5, 1), (0, 6, 1), (1, 7, 0), (1, 4, 1), (0, 5, 0)]
 
 
 def helpers(u, rack):
@@ -20,14 +20,11 @@ def helpers(u, rack):
 
 
 def sends(c, rack):
-    big, i = [], 0
-    for u in range(8):
-        if helpers(u, rack)[0] // 8 == c // 8:
-            big.append((u, 0xFF00))
-        else:
-            big.append((u, (1 << i) if i < 6 else 0xC0))
-            i += 1
-    return [big, [(8, 0x0F), (9, 0x30), (10, 0xC0)]]
+    on = [u for u in range(NU) if helpers(u, rack)[0] // 8 == c // 8]
+    off = [u for u in range(NU) if u not in on]
+    return [[(u, 1 << i) for i, u in enumerate(off[0:8])] + [(on[0], 0x0F00), (on[1], 0xF000)],
+            [(u, 1 << i) for i, u in enumerate(off[8:16])],
+            [(u, 3 << (2 * i)) for i, u in enumerate(off[16:20])]]
 
 
 def bits(m):
@@ -45,33 +42,34 @@ def rank_program(g, core, T, topo):
 
     if T.rank_of(core) is not None:
         k = peers.index(core)
-        g.sync.dma_start(T.pack[0:8], T.x3[:]).then_inc(S.ld3, 16)
-        g.scalar.dma_start(T.pack[8:10], T.x1[:]).then_inc(S.lds, 16)
-        g.sync.dma_start(T.pack[10, 0:64, :], T.x4[:]).then_inc(S.lds, 16)
-        g.scalar.dma_start(T.pack[10, 64:68, :], T.x2[:]).then_inc(S.lds, 16)
-        g.scalar.dma_start(T.pack[10, 68:128, :], T.x4[0:120, :]).then_inc(S.lds, 16)
+        g.sync.dma_start(T.pack[0:16], T.x3[:]).then_inc(S.ld3, 16)
+        g.scalar.dma_start(T.pack[16:20], T.x1[:]).then_inc(S.lds, 16)
+        g.sync.dma_start(T.pack[20], T.x4[:]).then_inc(S.lds, 16)
+        g.scalar.dma_start(T.pack[21, 0:8, :], T.x2[:]).then_inc(S.lds, 16)
+        g.scalar.dma_start(T.pack[21, 8:128, :], T.x4[0:120, :]).then_inc(S.lds, 16)
         out = 0
         for n, call in enumerate(sends(core, rack)):
             if n == 0:
                 g.wait_ge(S.ld3, 16)
-            else:
+            elif n == 1:
                 g.wait_ge(S.lds, 64)
             g.remote_dma_fused(
                 [RemoteDMATransfer(dst_ids=[did(helpers(u, rack)[0])], dma_engine_mask=m, remote_sem=S.in1,
                                    src=T.pack[u], dst=T.land[k]) for u, m in call],
                 local_sem=S.sent)
             out += sum(bits(m) for u, m in call)
-        g.sync.wait_ge(S.a3, 64)
-        g.sync.dma_start(T.y3[:], T.land[0:8]).then_inc(S.st, 16)
-        g.scalar.wait_ge(S.a1, 16)
-        g.scalar.dma_start(T.y1[:], T.land[8:10]).then_inc(S.st, 16)
-        g.scalar.wait_ge(S.a4, 8)
-        g.scalar.dma_start(T.y4[:], T.land[10, 0:64, :]).then_inc(S.st, 16)
-        g.scalar.dma_start(T.y2[:], T.land[10, 64:68, :]).then_inc(S.st, 16)
+        g.sync.wait_ge(S.a3, 128)
+        g.sync.dma_start(T.y3[:], T.land[0:16]).then_inc(S.st, 16)
+        g.scalar.wait_ge(S.a1, 32)
+        g.scalar.dma_start(T.y1[:], T.land[16:20]).then_inc(S.st, 16)
+        g.scalar.wait_ge(S.a4, 16)
+        g.scalar.dma_start(T.y4[:], T.land[20]).then_inc(S.st, 16)
+        g.sync.wait_ge(S.a4, 16)
+        g.sync.dma_start(T.y2[:], T.land[21, 0:8, :]).then_inc(S.st, 16)
         g.wait_ge(S.sent, out)
-        g.wait_ge(S.a3, 64)
-        g.wait_ge(S.a1, 16)
-        g.wait_ge(S.a4, 8)
+        g.wait_ge(S.a3, 128)
+        g.wait_ge(S.a1, 32)
+        g.wait_ge(S.a4, 16)
         g.wait_ge(S.st, 64)
         return
 
@@ -86,7 +84,7 @@ def rank_program(g, core, T, topo):
                 local_sem=S.sent)
             g.wait_ge(S.sent, 8)
         elif core == b:
-            arr = S.a3 if u < 8 else (S.a1 if u < 10 else S.a4)
+            arr = S.a3 if u < 16 else (S.a1 if u < 20 else S.a4)
             g.wait_ge(S.in2, 16)
             g.remote_dma_fused(
                 [RemoteDMATransfer(dst_ids=[did(c) for c in peers], dma_engine_mask=0xFF, remote_sem=arr,

@@ -7,9 +7,9 @@ SCRATCH = {
     "pack": ("dram", [NU, 128, U], "float32"),
     "land": ("dram", [NU, 128, U], "float32"),
 }
-SEMAPHORES = ["ld3", "lds", "sent", "in1", "in2", "a3", "a1", "a4", "st"]
+SEMAPHORES = ["ld3a", "ld3b", "lds", "sent", "in1", "in2", "a3a", "a3b", "a1", "a4", "st"]
 
-PLACE = [(s, c, d) for s in (0, 1) for c in (0, 1, 2, 3) for d in (0, 1)] + \
+PLACE = [(s, c, c % 2) for s in (0, 1) for c in (0, 1, 2, 3)] + [(s, c, 1 - c % 2) for s in (0, 1) for c in (0, 1, 2, 3)] + \
         [(0, 4, 0), (1, 5, 1), (0, 6, 1), (1, 7, 0), (1, 4, 1), (0, 5, 0)]
 
 
@@ -19,12 +19,17 @@ def helpers(u, rack):
     return (base + 5, base + 7) if die == 0 else (base + 1, base + 3)
 
 
+MASKS = [[0x01, 0x02, 0x04, 0x08, 0x10, 0x20, 0xC0],
+         [0x03, 0x04, 0x08, 0x10, 0x20, 0x40, 0x80],
+         [0x01, 0x02, 0x0C, 0x30, 0x40, 0x80]]
+
+
 def sends(c, rack):
-    on = [u for u in range(NU) if helpers(u, rack)[0] // 8 == c // 8]
-    off = [u for u in range(NU) if u not in on]
-    return [[(u, 1 << i) for i, u in enumerate(off[0:8])] + [(on[0], 0x0F00), (on[1], 0xF000)],
-            [(u, 1 << i) for i, u in enumerate(off[8:16])],
-            [(u, 3 << (2 * i)) for i, u in enumerate(off[16:20])]]
+    calls = []
+    for n, wave in enumerate((range(0, 8), range(8, 16), range(16, 22))):
+        off = [u for u in wave if helpers(u, rack)[0] // 8 != c // 8]
+        calls.append(list(zip(off, MASKS[n])) + [(u, 0xFF00) for u in wave if u not in off])
+    return calls
 
 
 def bits(m):
@@ -42,24 +47,24 @@ def rank_program(g, core, T, topo):
 
     if T.rank_of(core) is not None:
         k = peers.index(core)
-        g.sync.dma_start(T.pack[0:16], T.x3[:]).then_inc(S.ld3, 16)
-        g.scalar.dma_start(T.pack[16:20], T.x1[:]).then_inc(S.lds, 16)
-        g.sync.dma_start(T.pack[20], T.x4[:]).then_inc(S.lds, 16)
-        g.scalar.dma_start(T.pack[21, 0:8, :], T.x2[:]).then_inc(S.lds, 16)
+        g.sync.dma_start(T.pack[0:8], T.x3[0:64, :]).then_inc(S.ld3a, 16)
+        g.scalar.dma_start(T.pack[8:16], T.x3[64:128, :]).then_inc(S.ld3b, 16)
+        g.sync.dma_start(T.pack[16:20], T.x1[:]).then_inc(S.lds, 16)
+        g.scalar.dma_start(T.pack[20], T.x4[:]).then_inc(S.lds, 16)
+        g.sync.dma_start(T.pack[21, 0:8, :], T.x2[:]).then_inc(S.lds, 16)
         g.scalar.dma_start(T.pack[21, 8:128, :], T.x4[0:120, :]).then_inc(S.lds, 16)
         out = 0
-        for n, call in enumerate(sends(core, rack)):
-            if n == 0:
-                g.wait_ge(S.ld3, 16)
-            elif n == 1:
-                g.wait_ge(S.lds, 64)
+        for call, (sem, val) in zip(sends(core, rack), ((S.ld3a, 16), (S.ld3b, 16), (S.lds, 64))):
+            g.wait_ge(sem, val)
             g.remote_dma_fused(
                 [RemoteDMATransfer(dst_ids=[did(helpers(u, rack)[0])], dma_engine_mask=m, remote_sem=S.in1,
                                    src=T.pack[u], dst=T.land[k]) for u, m in call],
                 local_sem=S.sent)
             out += sum(bits(m) for u, m in call)
-        g.sync.wait_ge(S.a3, 128)
-        g.sync.dma_start(T.y3[:], T.land[0:16]).then_inc(S.st, 16)
+        g.sync.wait_ge(S.a3a, 64)
+        g.sync.dma_start(T.y3[0:64, :], T.land[0:8]).then_inc(S.st, 16)
+        g.sync.wait_ge(S.a3b, 64)
+        g.sync.dma_start(T.y3[64:128, :], T.land[8:16]).then_inc(S.st, 16)
         g.scalar.wait_ge(S.a1, 32)
         g.scalar.dma_start(T.y1[:], T.land[16:20]).then_inc(S.st, 16)
         g.scalar.wait_ge(S.a4, 16)
@@ -67,10 +72,11 @@ def rank_program(g, core, T, topo):
         g.sync.wait_ge(S.a4, 16)
         g.sync.dma_start(T.y2[:], T.land[21, 0:8, :]).then_inc(S.st, 16)
         g.wait_ge(S.sent, out)
-        g.wait_ge(S.a3, 128)
+        g.wait_ge(S.a3a, 64)
+        g.wait_ge(S.a3b, 64)
         g.wait_ge(S.a1, 32)
         g.wait_ge(S.a4, 16)
-        g.wait_ge(S.st, 64)
+        g.wait_ge(S.st, 80)
         return
 
     for u in range(NU):
@@ -84,7 +90,7 @@ def rank_program(g, core, T, topo):
                 local_sem=S.sent)
             g.wait_ge(S.sent, 8)
         elif core == b:
-            arr = S.a3 if u < 16 else (S.a1 if u < 20 else S.a4)
+            arr = S.a3a if u < 8 else (S.a3b if u < 16 else (S.a1 if u < 20 else S.a4))
             g.wait_ge(S.in2, 16)
             g.remote_dma_fused(
                 [RemoteDMATransfer(dst_ids=[did(c) for c in peers], dma_engine_mask=0xFF, remote_sem=arr,

from concourse.bass import DstId, RemoteDMATransfer

U = 16
NU = 22

SCRATCH = {
    "pack": ("dram", [NU, 128, U], "float32"),
    "land": ("dram", [NU, 128, U], "float32"),
}
SEMAPHORES = ["ld3a", "ld3b", "lds", "sent", "in1", "in2", "a3a", "a3b", "a1", "a4", "st"]

PLACE = [(s, c, c % 2) for s in (0, 1) for c in (0, 1, 2, 3)] + [(s, c, 1 - c % 2) for s in (0, 1) for c in (0, 1, 2, 3)] + \
        [(0, 4, 0), (1, 5, 1), (0, 6, 1), (1, 7, 0), (1, 4, 1), (0, 5, 0)]


def helpers(u, rack):
    slot, chip, die = PLACE[u]
    base = (slot if rack == 0 else 3 - slot) * 128 + chip * 8
    return (base + 5, base + 7) if die == 0 else (base + 1, base + 3)


MASKS = [[0x01, 0x02, 0x04, 0x08, 0x10, 0x20, 0xC0],
         [0x03, 0x04, 0x08, 0x10, 0x20, 0x40, 0x80],
         [0x01, 0x02, 0x0C, 0x30, 0x40, 0x80]]


def sends(c, rack):
    calls = []
    for n, wave in enumerate((range(0, 8), range(8, 16), range(16, 22))):
        off = [u for u in wave if helpers(u, rack)[0] // 8 != c // 8]
        calls.append(list(zip(off, MASKS[n])) + [(u, 0xFF00) for u in wave if u not in off])
    return calls


def bits(m):
    return bin(m).count("1")


def rank_program(g, core, T, topo):
    rack = topo.rack(topo.host(core))
    peers = [c for c in T.cores if topo.rack(topo.host(c)) == rack]
    S = T.sem

    def did(dst):
        rid, pid = topo.addr(dst, core)
        return DstId(rid=rid, pnc=pid)

    if T.rank_of(core) is not None:
        k = peers.index(core)
        g.sync.dma_start(T.pack[0:8], T.x3[0:64, :]).then_inc(S.ld3a, 16)
        g.scalar.dma_start(T.pack[8:16], T.x3[64:128, :]).then_inc(S.ld3b, 16)
        g.sync.dma_start(T.pack[16:20], T.x1[:]).then_inc(S.lds, 16)
        g.scalar.dma_start(T.pack[20], T.x4[:]).then_inc(S.lds, 16)
        g.sync.dma_start(T.pack[21, 0:8, :], T.x2[:]).then_inc(S.lds, 16)
        g.scalar.dma_start(T.pack[21, 8:128, :], T.x4[0:120, :]).then_inc(S.lds, 16)
        out = 0
        for call, (sem, val) in zip(sends(core, rack), ((S.ld3a, 16), (S.ld3b, 16), (S.lds, 64))):
            g.wait_ge(sem, val)
            g.remote_dma_fused(
                [RemoteDMATransfer(dst_ids=[did(helpers(u, rack)[0])], dma_engine_mask=m, remote_sem=S.in1,
                                   src=T.pack[u], dst=T.land[k]) for u, m in call],
                local_sem=S.sent)
            out += sum(bits(m) for u, m in call)
        g.sync.wait_ge(S.a3a, 64)
        g.sync.dma_start(T.y3[0:64, :], T.land[0:8]).then_inc(S.st, 16)
        g.sync.wait_ge(S.a3b, 64)
        g.sync.dma_start(T.y3[64:128, :], T.land[8:16]).then_inc(S.st, 16)
        g.scalar.wait_ge(S.a1, 32)
        g.scalar.dma_start(T.y1[:], T.land[16:20]).then_inc(S.st, 16)
        g.scalar.wait_ge(S.a4, 16)
        g.scalar.dma_start(T.y4[:], T.land[20]).then_inc(S.st, 16)
        g.sync.wait_ge(S.a4, 16)
        g.sync.dma_start(T.y2[:], T.land[21, 0:8, :]).then_inc(S.st, 16)
        g.wait_ge(S.sent, out)
        g.wait_ge(S.a3a, 64)
        g.wait_ge(S.a3b, 64)
        g.wait_ge(S.a1, 32)
        g.wait_ge(S.a4, 16)
        g.wait_ge(S.st, 80)
        return

    for u in range(NU):
        a, b = helpers(u, rack)
        if core == a:
            need = sum(bits(m) for c in peers for call in sends(c, rack) for v, m in call if v == u)
            g.wait_ge(S.in1, need)
            g.remote_dma_fused(
                [RemoteDMATransfer(dst_ids=[did(b), did(helpers(u, 1 - rack)[1])], dma_engine_mask=0xFF, remote_sem=S.in2,
                                   srcs=[T.land[j] for j in range(8)], dsts=[T.land[0], T.land[1]], alu_op=1)],
                local_sem=S.sent)
            g.wait_ge(S.sent, 8)
        elif core == b:
            arr = S.a3a if u < 8 else (S.a3b if u < 16 else (S.a1 if u < 20 else S.a4))
            g.wait_ge(S.in2, 16)
            g.remote_dma_fused(
                [RemoteDMATransfer(dst_ids=[did(c) for c in peers], dma_engine_mask=0xFF, remote_sem=arr,
                                   srcs=[T.land[0], T.land[1]], dsts=[T.land[u] for c in peers], alu_op=1)],
                local_sem=S.sent)
            g.wait_ge(S.sent, 8)
